import numpy as np, ml_dtypes
CORES = [36,164,52,180,100,228,116,244]
N = 8
KB, QP = 1, 64
ROOT = 6
def setup_inputs(rng):
    q = rng.standard_normal((N, 128, QP), dtype=np.float32) / 4; k = rng.standard_normal((N, 128, KB * 128), dtype=np.float32)
    a = 2 * np.pi * rng.random((N, QP)); s = 400 * rng.random((N, QP)) ** 1.5; q[:, 0, :] = s * np.cos(a); q[:, 1, :] = s * np.sin(a); q[:, 2, :] = 150 * rng.standard_normal((N, QP)); k[:, 2, :] = 1 + k[:, 2, :] / 50
    a = (2 * np.pi * rng.random() + np.pi / 2 * (rng.permutation(N).reshape(N, 1, 1) + 0.5) / N - 0.5 + (np.arange(KB).reshape(1, KB, 1) + rng.random((N, KB, 128))) / KB).reshape(N, KB * 128); k[:, 0, :] = np.cos(a); k[:, 1, :] = np.sin(a)
    for t in range(0, QP, 2):
        j, i = (t // 2) % N, rng.integers(KB * 128); q[ROOT, :2, t] = s[ROOT, t] * k[j, :2, i]; q[ROOT, 3:, t] += k[j, 3:, i] / 8
    return {"q": q.astype(ml_dtypes.bfloat16), "k": k.astype(ml_dtypes.bfloat16), "v": rng.standard_normal((N, 128, KB * 128), dtype=np.float32).astype(ml_dtypes.bfloat16)}
def setup_inputs_big(rng):
    d = setup_inputs(rng)
    for k in ("v",): d[k] = (d[k].astype(np.float32) * 1048576.0).astype(d[k].dtype)
    return d
def setup_inputs_small(rng):
    d = setup_inputs(rng)
    for k in ("v",): d[k] = (d[k].astype(np.float32) * (1 / 1048576.0)).astype(d[k].dtype)
    return d
def reference(q, k, v):
    Q, K, V = q.astype(np.float64), k.astype(np.float64), v.astype(np.float64)
    y = np.full((N, QP, 128), np.nan)
    for r in [ROOT]:
        js = list(range(N))
        S = np.concatenate([K[j].T @ Q[r] for j in js], axis=0)
        P = np.exp(S - S.max(axis=0)); P = P / P.sum(axis=0)
        y[r] = P.T @ np.concatenate([V[j][:, 128 * b:128 * b + 128] for j in js for b in range(KB)], axis=0)
    return {"y": y.astype(ml_dtypes.bfloat16)}

@@ -1,0 +1,149 @@
+from concourse.mybir import AluOpType, AxisListType, ActivationFunctionType
+
+KP, QP, F = 128, 64, 128
+NR = 8
+G = 4
+PER = NR // G
+H = 2
+PH = NR // H
+
+SCRATCH = {
+    "kd": ("dram", [128, KP], "bfloat16"),
+    "vd": ("dram", [128, F], "bfloat16"),
+    "qs": ("sbuf", [128, QP], "bfloat16"),
+    "K": ("sbuf", [128, NR * KP], "bfloat16"),
+    "V": ("sbuf", [128, NR * F], "bfloat16"),
+    "PT": ("sbuf", [128, NR * QP], "bfloat16"),
+    "zer": ("sbuf", [128, PH * QP], "bfloat16"),
+    "ones": ("sbuf", [128, 128], "bfloat16"),
+    "I": ("sbuf", [128, 128], "bfloat16"),
+    "mg": ("sbuf", [128, G], "float32"),
+    "negm": ("sbuf", [128, 1], "float32"),
+    "diag": ("sbuf", [128, QP], "bfloat16"),
+    "rl": ("sbuf", [128, 1], "float32"),
+    "yT": ("sbuf", [128, QP], "bfloat16"),
+    "yb": ("sbuf", [128, F], "bfloat16"),
+    "S0": ("psum", [128, 512], "float32"),
+    "S1": ("psum", [128, 512], "float32"),
+    "S2": ("psum", [128, 512], "float32"),
+    "S3": ("psum", [128, 512], "float32"),
+    "ST0": ("psum", [128, 512], "float32"),
+    "ST1": ("psum", [128, 512], "float32"),
+    "L": ("psum", [128, 512], "float32"),
+    "OT": ("psum", [128, 512], "float32"),
+}
+SEMAPHORES = (["ql", "kl", "vl", "sent", "cz", "c1", "ci", "sm", "sn", "sd", "sl", "sr", "so", "syt", "sy", "syb", "done"]
+              + ["ka%d" % i for i in range(G)] + ["va%d" % i for i in range(NR)] + ["ss%d" % i for i in range(G)]
+              + ["st%d" % i for i in range(H)] + ["sp%d" % i for i in range(H)])
+
+
+def _count(mask):
+    return bin(mask).count("1")
+
+
+def _sender(g, core, rank, T, topo, rc):
+    sem = T.sem
+    mask = topo.mask(core, rc)
+    rid, pid = topo.addr(rc, core)
+    g.sync.dma_start(T.kd[:], T.k[:]).then_inc(sem.kl, 16)
+    g.scalar.dma_start(T.vd[:], T.v[:]).then_inc(sem.vl, 16)
+    g.wait_ge(sem.kl, 16)
+    g.remote_dma(out_ap=T.K[:, rank * KP:(rank + 1) * KP], in_ap=T.kd[:], remote_sem=sem["ka%d" % (rank // PER)],
+                 local_sem=sem.sent, pid=pid, routing_id=rid, dma_engine_mask=mask)
+    g.wait_ge(sem.vl, 16)
+    g.remote_dma(out_ap=T.V[:, rank * F:(rank + 1) * F], in_ap=T.vd[:], remote_sem=sem["va%d" % rank],
+                 local_sem=sem.sent, pid=pid, routing_id=rid, dma_engine_mask=mask)
+    g.wait_ge(sem.sent, 2 * _count(mask))
+
+
+def _root(g, core, root, T, topo):
+    sem = T.sem
+    te, ve, se = g.tensor, g.vector, g.scalar
+    Exp = ActivationFunctionType.Exp
+    X, mx, mult = AxisListType.X, AluOpType.max, AluOpType.mult
+    eng = [0 if j == root else _count(topo.mask(T.cores[j], core)) for j in range(NR)]
+    S = [T["S%d" % i] for i in range(G)]
+    ST = [T["ST%d" % i] for i in range(H)]
+    Y = S[0]
+
+    g.sync.dma_start(T.qs[:], T.q[:]).then_inc(sem.ql, 16)
+    se.dma_start(T.K[:, root * KP:(root + 1) * KP], T.k[:]).then_inc(sem.kl, 16)
+    g.sync.dma_start(T.V[:, root * F:(root + 1) * F], T.v[:]).then_inc(sem.vl, 16)
+
+    ve.memset(T.zer[:], 0.0).then_inc(sem.cz, 1)
+    se.wait_ge(sem.cz, 1)
+    se.activation(T.ones[:], T.zer[:, 0:128], Exp).then_inc(sem.c1, 1)
+    g.wait_ge(sem.c1, 1)
+    g.affine_select(T.I[:], T.ones[:], [[-1, 128]], AluOpType.is_equal, 0.0, 0, 1).then_inc(sem.ci, 1)
+
+    te.wait_ge(sem.cz, 1)
+    for h in range(H):
+        te.matmul(ST[h][:, 0:PH * QP], T.zer[:, 0:128], T.zer[:, 0:PH * QP], True, False)
+    te.wait_ge(sem.ql, 16)
+    for i in range(G):
+        members = range(i * PER, (i + 1) * PER)
+        te.wait_ge(sem["ka%d" % i], sum(eng[j] for j in members))
+        if root in members:
+            te.wait_ge(sem.kl, 16)
+        te.matmul(S[i][0:QP, 0:PER * KP], T.qs[:], T.K[:, i * PER * KP:(i + 1) * PER * KP], True, True
+                  ).then_inc(sem["ss%d" % i], 1)
+    for j in range(NR):
+        h, c = divmod(j, PH)
+        te.matmul(ST[h][:, c * QP:(c + 1) * QP], T.K[:, j * KP:(j + 1) * KP], T.qs[:], False, False)
+
+    for i in range(G):
+        ve.wait_ge(sem["ss%d" % i], 1)
+        ve.tensor_reduce(T.mg[0:QP, i:i + 1], S[i][0:QP, 0:PER * KP], X, mx).then_inc(sem.sm, 1)
+    ve.wait_ge(sem.sm, G)
+    ve.tensor_reduce(T.negm[0:QP, 0:1], T.mg[0:QP, 0:G], X, mx, negate=True).then_inc(sem.sn, 1)
+    ve.wait_ge(sem.sn, 1)
+    ve.wait_ge(sem.ci, 1)
+    ve.tensor_scalar(T.diag[0:QP, 0:QP], T.I[0:QP, 0:QP], T.negm[0:QP, 0:1], None, mult).then_inc(sem.sd, 1)
+
+    te.wait_ge(sem.sd, 1)
+    te.wait_ge(sem.c1, 1)
+    for j in range(NR):
+        h, c = divmod(j, PH)
+        te.matmul(ST[h][:, c * QP:(c + 1) * QP], T.ones[0:QP, 0:128], T.diag[0:QP, 0:QP], False, c == PH - 1
+                  ).then_inc(sem["st%d" % h], 1)
+
+    for h in range(H):
+        se.wait_ge(sem["st%d" % h], PH)
+        se.activation(T.PT[:, h * PH * QP:(h + 1) * PH * QP], ST[h][:, 0:PH * QP], Exp).then_inc(sem["sp%d" % h], 1)
+
+    for j in range(NR):
+        if j % PH == 0:
+            te.wait_ge(sem["sp%d" % (j // PH)], 1)
+        te.matmul(T.L[0:QP, 0:1], T.PT[:, j * QP:(j + 1) * QP], T.ones[:, 0:1], j == 0, j == NR - 1).then_inc(sem.sl, 1)
+    order = [root] + [j for j in range(NR) if j != root]
+    for i, j in enumerate(order):
+        if j == root:
+            te.wait_ge(sem.vl, 16)
+        else:
+            te.wait_ge(sem["va%d" % j], eng[j])
+        te.matmul(T.OT[:, 0:QP], T.V[:, j * F:(j + 1) * F], T.PT[:, j * QP:(j + 1) * QP], i == 0, i == NR - 1
+                  ).then_inc(sem.so, 1)
+
+    ve.wait_ge(sem.sl, NR)
+    ve.reciprocal(T.rl[0:QP, 0:1], T.L[0:QP, 0:1]).then_inc(sem.sr, 1)
+    ve.wait_ge(sem.so, NR)
+    ve.tensor_copy(T.yT[:, 0:QP], T.OT[:, 0:QP]).then_inc(sem.syt, 1)
+    te.wait_ge(sem.syt, 1)
+    te.wait_ge(sem.ci, 1)
+    te.matmul(Y[0:QP, 0:F], T.yT[:, 0:QP], T.I[:, 0:F], True, True).then_inc(sem.sy, 1)
+    ve.wait_ge(sem.sy, 1)
+    ve.wait_ge(sem.sr, 1)
+    ve.tensor_scalar(T.yb[0:QP, 0:F], Y[0:QP, 0:F], T.rl[0:QP, 0:1], None, mult).then_inc(sem.syb, 1)
+    g.sync.wait_ge(sem.syb, 1)
+    g.sync.dma_start(T.y[:], T.yb[0:QP, :]).then_inc(sem.done, 16)
+    g.sync.wait_ge(sem.done, 16)
+
+
+def rank_program(g, core, T, topo):
+    rank = T.rank_of(core)
+    if rank is None:
+        return
+    if rank == T.root:
+        _root(g, core, rank, T, topo)
+    else:
+        _sender(g, core, rank, T, topo, T.cores[T.root])

@@ -2,26 +2,26 @@ from concourse.mybir import AluOpType, AxisListType, ActivationFunctionType
 
 KP, QP, F = 128, 64, 128
 NR = 8
-G = 4
-PER = NR // G
-H = 2
-PH = NR // H
+FH = F // 2
+OWN = NR - 1
+NB = 4
+VS = FH + 8
 
 SCRATCH = {
     "kd": ("dram", [128, KP], "bfloat16"),
-    "vd": ("dram", [128, F], "bfloat16"),
+    "vs": ("sbuf", [128, F], "bfloat16"),
     "qs": ("sbuf", [128, QP], "bfloat16"),
     "K": ("sbuf", [128, NR * KP], "bfloat16"),
-    "V": ("sbuf", [128, NR * F], "bfloat16"),
+    "Vlo": ("sbuf", [128, NR * VS], "bfloat16"),
+    "Vhi": ("sbuf", [128, NR * FH], "bfloat16"),
     "PT": ("sbuf", [128, NR * QP], "bfloat16"),
-    "zer": ("sbuf", [128, PH * QP], "bfloat16"),
+    "zer": ("sbuf", [128, 128], "bfloat16"),
     "ones": ("sbuf", [128, 128], "bfloat16"),
     "I": ("sbuf", [128, 128], "bfloat16"),
-    "mg": ("sbuf", [128, G], "float32"),
+    "mg": ("sbuf", [128, NR], "float32"),
     "negm": ("sbuf", [128, 1], "float32"),
     "diag": ("sbuf", [128, QP], "bfloat16"),
     "rl": ("sbuf", [128, 1], "float32"),
-    "yT": ("sbuf", [128, QP], "bfloat16"),
     "yb": ("sbuf", [128, F], "bfloat16"),
     "S0": ("psum", [128, 512], "float32"),
     "S1": ("psum", [128, 512], "float32"),
@@ -29,112 +29,145 @@ SCRATCH = {
     "S3": ("psum", [128, 512], "float32"),
     "ST0": ("psum", [128, 512], "float32"),
     "ST1": ("psum", [128, 512], "float32"),
-    "L": ("psum", [128, 512], "float32"),
-    "OT": ("psum", [128, 512], "float32"),
+    "ST2": ("psum", [128, 512], "float32"),
+    "ST3": ("psum", [128, 512], "float32"),
 }
-SEMAPHORES = (["ql", "kl", "vl", "sent", "cz", "c1", "ci", "sm", "sn", "sd", "sl", "sr", "so", "syt", "sy", "syb", "done"]
-              + ["ka%d" % i for i in range(G)] + ["va%d" % i for i in range(NR)] + ["ss%d" % i for i in range(G)]
-              + ["st%d" % i for i in range(H)] + ["sp%d" % i for i in range(H)])
+SEMAPHORES = (["ql", "kl", "vl", "vl2", "sent", "cz", "c1", "c2", "ci", "sso", "smo", "sn", "sd", "slo", "shi", "sr",
+               "syb", "done"]
+              + ["ka%d" % i for i in range(NR - 1)] + ["ss%d" % i for i in range(NR - 1)] + ["rm%d" % i for i in range(NR - 1)]
+              + ["va%d" % i for i in range(NR - 1)] + ["vb%d" % i for i in range(NR - 1)]
+              + ["st%d" % i for i in range(NB)] + ["sp%d" % i for i in range(NB)])
 
 
 def _count(mask):
     return bin(mask).count("1")
 
 
-def _sender(g, core, rank, T, topo, rc):
+def _half(mask):
+    bits = [b for b in range(mask.bit_length()) if (mask >> b) & 1]
+    out = 0
+    for b in bits[::2]:
+        out |= 1 << b
+    return out
+
+
+def _sender(g, core, slot, T, topo, rc):
     sem = T.sem
-    mask = topo.mask(core, rc)
+    mask = _half(topo.mask(core, rc))
     rid, pid = topo.addr(rc, core)
     g.sync.dma_start(T.kd[:], T.k[:]).then_inc(sem.kl, 16)
-    g.scalar.dma_start(T.vd[:], T.v[:]).then_inc(sem.vl, 16)
+    g.sync.dma_start(T.vs[:], T.v[:]).then_inc(sem.vl, 16)
     g.wait_ge(sem.kl, 16)
-    g.remote_dma(out_ap=T.K[:, rank * KP:(rank + 1) * KP], in_ap=T.kd[:], remote_sem=sem["ka%d" % (rank // PER)],
+    g.remote_dma(out_ap=T.K[:, slot * KP:(slot + 1) * KP], in_ap=T.kd[:], remote_sem=sem["ka%d" % slot],
                  local_sem=sem.sent, pid=pid, routing_id=rid, dma_engine_mask=mask)
     g.wait_ge(sem.vl, 16)
-    g.remote_dma(out_ap=T.V[:, rank * F:(rank + 1) * F], in_ap=T.vd[:], remote_sem=sem["va%d" % rank],
+    g.remote_dma(out_ap=T.Vlo[:, slot * VS:slot * VS + FH], in_ap=T.vs[:, 0:FH], remote_sem=sem["va%d" % slot],
                  local_sem=sem.sent, pid=pid, routing_id=rid, dma_engine_mask=mask)
-    g.wait_ge(sem.sent, 2 * _count(mask))
+    g.remote_dma(out_ap=T.Vhi[:, slot * FH:(slot + 1) * FH], in_ap=T.vs[:, FH:F], remote_sem=sem["vb%d" % slot],
+                 local_sem=sem.sent, pid=pid, routing_id=rid, dma_engine_mask=mask)
+    g.wait_ge(sem.sent, 3 * _count(mask))
 
 
-def _root(g, core, root, T, topo):
+def _root(g, core, T, topo, others):
     sem = T.sem
     te, ve, se = g.tensor, g.vector, g.scalar
     Exp = ActivationFunctionType.Exp
     X, mx, mult = AxisListType.X, AluOpType.max, AluOpType.mult
-    eng = [0 if j == root else _count(topo.mask(T.cores[j], core)) for j in range(NR)]
-    S = [T["S%d" % i] for i in range(G)]
-    ST = [T["ST%d" % i] for i in range(H)]
-    Y = S[0]
+    eng = [_count(_half(topo.mask(T.cores[j], core))) for j in others]
+    S = [T["S%d" % i] for i in range(NB)]
+    ST = [T["ST%d" % i] for i in range(NB)]
+    Olo, Ohi = S[1], S[2]
+
+    def sb(s):
+        return S[(s + 1) % NB][0:QP, 0:KP]
+
+    def st(s):
+        c = (s // NB) * QP
+        return ST[s % NB][:, c:c + QP]
+
+    def pt(s):
+        c = (2 * (s % NB) + s // NB) * QP
+        return T.PT[:, c:c + QP]
+
+    def ks(s):
+        return T.K[:, s * KP:(s + 1) * KP]
 
     g.sync.dma_start(T.qs[:], T.q[:]).then_inc(sem.ql, 16)
-    se.dma_start(T.K[:, root * KP:(root + 1) * KP], T.k[:]).then_inc(sem.kl, 16)
-    g.sync.dma_start(T.V[:, root * F:(root + 1) * F], T.v[:]).then_inc(sem.vl, 16)
+    se.dma_start(ks(OWN), T.k[:]).then_inc(sem.kl, 16)
+    g.sync.dma_start(T.Vlo[:, OWN * VS:OWN * VS + FH], T.v[:, 0:FH]).then_inc(sem.vl, 16)
+    se.dma_start(T.Vhi[:, OWN * FH:(OWN + 1) * FH], T.v[:, FH:F]).then_inc(sem.vl2, 16)
 
     ve.memset(T.zer[:], 0.0).then_inc(sem.cz, 1)
+    for s in range(NR):
+        ve.memset(T.Vlo[:, s * VS + FH:(s + 1) * VS], 1.0).then_inc(sem.c2, 1)
     se.wait_ge(sem.cz, 1)
-    se.activation(T.ones[:], T.zer[:, 0:128], Exp).then_inc(sem.c1, 1)
+    se.activation(T.ones[:], T.zer[:], Exp).then_inc(sem.c1, 1)
     g.wait_ge(sem.c1, 1)
     g.affine_select(T.I[:], T.ones[:], [[-1, 128]], AluOpType.is_equal, 0.0, 0, 1).then_inc(sem.ci, 1)
 
     te.wait_ge(sem.cz, 1)
-    for h in range(H):
-        te.matmul(ST[h][:, 0:PH * QP], T.zer[:, 0:128], T.zer[:, 0:PH * QP], True, False)
+    for i in range(NB):
+        te.matmul(ST[i][:, 0:2 * QP], T.zer[:], T.zer[:, 0:2 * QP], True, False)
     te.wait_ge(sem.ql, 16)
-    for i in range(G):
-        members = range(i * PER, (i + 1) * PER)
-        te.wait_ge(sem["ka%d" % i], sum(eng[j] for j in members))
-        if root in members:
-            te.wait_ge(sem.kl, 16)
-        te.matmul(S[i][0:QP, 0:PER * KP], T.qs[:], T.K[:, i * PER * KP:(i + 1) * PER * KP], True, True
-                  ).then_inc(sem["ss%d" % i], 1)
-    for j in range(NR):
-        h, c = divmod(j, PH)
-        te.matmul(ST[h][:, c * QP:(c + 1) * QP], T.K[:, j * KP:(j + 1) * KP], T.qs[:], False, False)
+    te.wait_ge(sem.kl, 16)
+    te.matmul(S[0][0:QP, 0:KP], T.qs[:], ks(OWN), True, True).then_inc(sem.sso, 1)
+    te.matmul(st(OWN), ks(OWN), T.qs[:], False, False)
+    for s in range(NR - 1):
+        te.wait_ge(sem["ka%d" % s], eng[s])
+        if s == NB - 1:
+            te.wait_ge(sem.smo, 1)
+        elif s >= NB:
+            te.wait_ge(sem["rm%d" % (s - NB)], 1)
+        te.matmul(sb(s), T.qs[:], ks(s), True, True).then_inc(sem["ss%d" % s], 1)
+    for s in range(NR - 1):
+        te.matmul(st(s), ks(s), T.qs[:], False, False)
 
-    for i in range(G):
-        ve.wait_ge(sem["ss%d" % i], 1)
-        ve.tensor_reduce(T.mg[0:QP, i:i + 1], S[i][0:QP, 0:PER * KP], X, mx).then_inc(sem.sm, 1)
-    ve.wait_ge(sem.sm, G)
-    ve.tensor_reduce(T.negm[0:QP, 0:1], T.mg[0:QP, 0:G], X, mx, negate=True).then_inc(sem.sn, 1)
+    ve.wait_ge(sem.sso, 1)
+    ve.tensor_reduce(T.mg[0:QP, 0:1], S[0][0:QP, 0:KP], X, mx).then_inc(sem.smo, 1)
+    for s in range(NR - 1):
+        ve.wait_ge(sem["ss%d" % s], 1)
+        ve.tensor_reduce(T.mg[0:QP, s + 1:s + 2], sb(s), X, mx).then_inc(sem["rm%d" % s], 1)
+    ve.wait_ge(sem.smo, 1)
+    for s in range(NR - 1):
+        ve.wait_ge(sem["rm%d" % s], 1)
+    ve.tensor_reduce(T.negm[0:QP, 0:1], T.mg[0:QP, 0:NR], X, mx, negate=True).then_inc(sem.sn, 1)
     ve.wait_ge(sem.sn, 1)
     ve.wait_ge(sem.ci, 1)
     ve.tensor_scalar(T.diag[0:QP, 0:QP], T.I[0:QP, 0:QP], T.negm[0:QP, 0:1], None, mult).then_inc(sem.sd, 1)
 
     te.wait_ge(sem.sd, 1)
     te.wait_ge(sem.c1, 1)
-    for j in range(NR):
-        h, c = divmod(j, PH)
-        te.matmul(ST[h][:, c * QP:(c + 1) * QP], T.ones[0:QP, 0:128], T.diag[0:QP, 0:QP], False, c == PH - 1
-                  ).then_inc(sem["st%d" % h], 1)
+    for i in range(NB):
+        for s in (i, i + NB):
+            te.matmul(st(s), T.ones[0:QP, 0:128], T.diag[0:QP, 0:QP], False, s >= NB).then_inc(sem["st%d" % i], 1)
+    for i in range(NB):
+        se.wait_ge(sem["st%d" % i], 2)
+        se.activation(T.PT[:, 2 * i * QP:(2 * i + 2) * QP], ST[i][:, 0:2 * QP], Exp).then_inc(sem["sp%d" % i], 1)
 
-    for h in range(H):
-        se.wait_ge(sem["st%d" % h], PH)
-        se.activation(T.PT[:, h * PH * QP:(h + 1) * PH * QP], ST[h][:, 0:PH * QP], Exp).then_inc(sem["sp%d" % h], 1)
-
-    for j in range(NR):
-        if j % PH == 0:
-            te.wait_ge(sem["sp%d" % (j // PH)], 1)
-        te.matmul(T.L[0:QP, 0:1], T.PT[:, j * QP:(j + 1) * QP], T.ones[:, 0:1], j == 0, j == NR - 1).then_inc(sem.sl, 1)
-    order = [root] + [j for j in range(NR) if j != root]
-    for i, j in enumerate(order):
-        if j == root:
+    order = [s for i in range(NB) for s in (i, i + NB)]
+    te.wait_ge(sem.c2, NR)
+    for n, s in enumerate(order):
+        if s < NB:
+            te.wait_ge(sem["sp%d" % s], 1)
+        if s == OWN:
             te.wait_ge(sem.vl, 16)
         else:
-            te.wait_ge(sem["va%d" % j], eng[j])
-        te.matmul(T.OT[:, 0:QP], T.V[:, j * F:(j + 1) * F], T.PT[:, j * QP:(j + 1) * QP], i == 0, i == NR - 1
-                  ).then_inc(sem.so, 1)
+            te.wait_ge(sem["va%d" % s], eng[s])
+        te.matmul(Olo[0:QP, 0:FH + 1], pt(s), T.Vlo[:, s * VS:s * VS + FH + 1], n == 0, n == NR - 1).then_inc(sem.slo, 1)
+    for n, s in enumerate(order):
+        if s == OWN:
+            te.wait_ge(sem.vl2, 16)
+        else:
+            te.wait_ge(sem["vb%d" % s], eng[s])
+        te.matmul(Ohi[0:QP, 0:FH], pt(s), T.Vhi[:, s * FH:(s + 1) * FH], n == 0, n == NR - 1).then_inc(sem.shi, 1)
 
-    ve.wait_ge(sem.sl, NR)
-    ve.reciprocal(T.rl[0:QP, 0:1], T.L[0:QP, 0:1]).then_inc(sem.sr, 1)
-    ve.wait_ge(sem.so, NR)
-    ve.tensor_copy(T.yT[:, 0:QP], T.OT[:, 0:QP]).then_inc(sem.syt, 1)
-    te.wait_ge(sem.syt, 1)
-    te.wait_ge(sem.ci, 1)
-    te.matmul(Y[0:QP, 0:F], T.yT[:, 0:QP], T.I[:, 0:F], True, True).then_inc(sem.sy, 1)
-    ve.wait_ge(sem.sy, 1)
+    ve.wait_ge(sem.slo, NR)
+    ve.reciprocal(T.rl[0:QP, 0:1], Olo[0:QP, FH:FH + 1]).then_inc(sem.sr, 1)
     ve.wait_ge(sem.sr, 1)
-    ve.tensor_scalar(T.yb[0:QP, 0:F], Y[0:QP, 0:F], T.rl[0:QP, 0:1], None, mult).then_inc(sem.syb, 1)
-    g.sync.wait_ge(sem.syb, 1)
+    ve.tensor_scalar(T.yb[0:QP, 0:FH], Olo[0:QP, 0:FH], T.rl[0:QP, 0:1], None, mult).then_inc(sem.syb, 1)
+    ve.wait_ge(sem.shi, NR)
+    ve.tensor_scalar(T.yb[0:QP, FH:F], Ohi[0:QP, 0:FH], T.rl[0:QP, 0:1], None, mult).then_inc(sem.syb, 1)
+    g.sync.wait_ge(sem.syb, 2)
     g.sync.dma_start(T.y[:], T.yb[0:QP, :]).then_inc(sem.done, 16)
     g.sync.wait_ge(sem.done, 16)
 
@@ -143,7 +176,8 @@ def rank_program(g, core, T, topo):
     rank = T.rank_of(core)
     if rank is None:
         return
+    others = [j for j in range(NR) if j != T.root]
     if rank == T.root:
-        _root(g, core, rank, T, topo)
+        _root(g, core, T, topo, others)
     else:
-        _sender(g, core, rank, T, topo, T.cores[T.root])
+        _sender(g, core, others.index(rank), T, topo, T.cores[T.root])

@@ -5,22 +5,25 @@ NR = 8
 FH = F // 2
 OWN = NR - 1
 NB = 4
-VS = FH + 8
+LOW = -1e29
+OB = 8
+VS = FH + OB
 
 SCRATCH = {
     "kd": ("dram", [128, KP], "bfloat16"),
     "vs": ("sbuf", [128, F], "bfloat16"),
+    "on": ("sbuf", [128, OB], "bfloat16"),
     "qs": ("sbuf", [128, QP], "bfloat16"),
     "K": ("sbuf", [128, NR * KP], "bfloat16"),
     "Vlo": ("sbuf", [128, NR * VS], "bfloat16"),
     "Vhi": ("sbuf", [128, NR * FH], "bfloat16"),
     "PT": ("sbuf", [128, NR * QP], "bfloat16"),
     "zer": ("sbuf", [128, 128], "bfloat16"),
-    "ones": ("sbuf", [128, 128], "bfloat16"),
-    "I": ("sbuf", [128, 128], "bfloat16"),
-    "mg": ("sbuf", [128, NR], "float32"),
-    "negm": ("sbuf", [128, 1], "float32"),
-    "diag": ("sbuf", [128, QP], "bfloat16"),
+    "ones": ("sbuf", [128, QP], "bfloat16"),
+    "nones": ("sbuf", [128, QP], "bfloat16"),
+    "NI": ("sbuf", [128, QP], "bfloat16"),
+    "mg": ("sbuf", [128, 2 * KP], "float32"),
+    "Cb": ("sbuf", [128, 2 * KP], "bfloat16"),
     "rl": ("sbuf", [128, 1], "float32"),
     "yb": ("sbuf", [128, F], "bfloat16"),
     "S0": ("psum", [128, 512], "float32"),
@@ -32,9 +35,9 @@ SCRATCH = {
     "ST2": ("psum", [128, 512], "float32"),
     "ST3": ("psum", [128, 512], "float32"),
 }
-SEMAPHORES = (["ql", "kl", "vl", "vl2", "sent", "cz", "c1", "c2", "ci", "sso", "smo", "sn", "sd", "slo", "shi", "sr",
-               "syb", "done"]
-              + ["ka%d" % i for i in range(NR - 1)] + ["ss%d" % i for i in range(NR - 1)] + ["rm%d" % i for i in range(NR - 1)]
+SEMAPHORES = (["ql", "kl", "vl", "vl2", "sent", "cz", "c1", "c2", "ci", "cn", "cp", "sso", "smo", "sd", "slo", "shi", "sr",
+               "syb", "syh", "done", "done2"]
+              + ["ka%d" % i for i in range(NR - 1)] + ["ss%d" % i for i in range(NR - 1)] + ["rm%d" % i for i in range(NR - 2)]
               + ["va%d" % i for i in range(NR - 1)] + ["vb%d" % i for i in range(NR - 1)]
               + ["st%d" % i for i in range(NB)] + ["sp%d" % i for i in range(NB)])
 
@@ -43,20 +46,16 @@ def _count(mask):
     return bin(mask).count("1")
 
 
-def _half(mask):
-    bits = [b for b in range(mask.bit_length()) if (mask >> b) & 1]
-    out = 0
-    for b in bits[::2]:
-        out |= 1 << b
-    return out
-
-
 def _sender(g, core, slot, T, topo, rc):
     sem = T.sem
-    mask = _half(topo.mask(core, rc))
+    mask = topo.mask(core, rc)
     rid, pid = topo.addr(rc, core)
     g.sync.dma_start(T.kd[:], T.k[:]).then_inc(sem.kl, 16)
     g.sync.dma_start(T.vs[:], T.v[:]).then_inc(sem.vl, 16)
+    g.vector.memset(T.on[:], 1.0).then_inc(sem.c2, 1)
+    g.wait_ge(sem.c2, 1)
+    g.remote_dma(out_ap=T.Vlo[:, slot * VS + FH:(slot + 1) * VS], in_ap=T.on[:], remote_sem=sem["va%d" % slot],
+                 local_sem=sem.sent, pid=pid, routing_id=rid, dma_engine_mask=mask)
     g.wait_ge(sem.kl, 16)
     g.remote_dma(out_ap=T.K[:, slot * KP:(slot + 1) * KP], in_ap=T.kd[:], remote_sem=sem["ka%d" % slot],
                  local_sem=sem.sent, pid=pid, routing_id=rid, dma_engine_mask=mask)
@@ -65,7 +64,7 @@ def _sender(g, core, slot, T, topo, rc):
                  local_sem=sem.sent, pid=pid, routing_id=rid, dma_engine_mask=mask)
     g.remote_dma(out_ap=T.Vhi[:, slot * FH:(slot + 1) * FH], in_ap=T.vs[:, FH:F], remote_sem=sem["vb%d" % slot],
                  local_sem=sem.sent, pid=pid, routing_id=rid, dma_engine_mask=mask)
-    g.wait_ge(sem.sent, 3 * _count(mask))
+    g.wait_ge(sem.sent, 4 * _count(mask))
 
 
 def _root(g, core, T, topo, others):
@@ -73,10 +72,11 @@ def _root(g, core, T, topo, others):
     te, ve, se = g.tensor, g.vector, g.scalar
     Exp = ActivationFunctionType.Exp
     X, mx, mult = AxisListType.X, AluOpType.max, AluOpType.mult
-    eng = [_count(_half(topo.mask(T.cores[j], core))) for j in others]
+    eng = [_count(topo.mask(T.cores[j], core)) for j in others]
     S = [T["S%d" % i] for i in range(NB)]
     ST = [T["ST%d" % i] for i in range(NB)]
     Olo, Ohi = S[1], S[2]
+    LB = (NR - 1) % NB
 
     def sb(s):
         return S[(s + 1) % NB][0:QP, 0:KP]
@@ -98,14 +98,18 @@ def _root(g, core, T, topo, others):
     se.dma_start(T.Vhi[:, OWN * FH:(OWN + 1) * FH], T.v[:, FH:F]).then_inc(sem.vl2, 16)
 
     ve.memset(T.zer[:], 0.0).then_inc(sem.cz, 1)
-    for s in range(NR):
-        ve.memset(T.Vlo[:, s * VS + FH:(s + 1) * VS], 1.0).then_inc(sem.c2, 1)
+    ve.memset(T.mg[0:QP, NR - 1:2 * KP], LOW).then_inc(sem.cp, 1)
+    ve.memset(S[LB][0:QP, KP:2 * KP], LOW).then_inc(sem.cp, 1)
+    ve.memset(T.Vlo[:, OWN * VS + FH:(OWN + 1) * VS], 1.0).then_inc(sem.c2, 1)
     se.wait_ge(sem.cz, 1)
-    se.activation(T.ones[:], T.zer[:], Exp).then_inc(sem.c1, 1)
-    g.wait_ge(sem.c1, 1)
-    g.affine_select(T.I[:], T.ones[:], [[-1, 128]], AluOpType.is_equal, 0.0, 0, 1).then_inc(sem.ci, 1)
+    se.activation(T.ones[0:QP, :], T.zer[0:QP, 0:QP], Exp).then_inc(sem.c1, 1)
+    ve.wait_ge(sem.c1, 1)
+    ve.tensor_scalar(T.nones[0:QP, :], T.ones[0:QP, :], -1.0, None, mult).then_inc(sem.cn, 1)
+    g.wait_ge(sem.cn, 1)
+    g.affine_select(T.NI[0:QP, :], T.nones[0:QP, :], [[-1, QP]], AluOpType.is_equal, 0.0, 0, 1).then_inc(sem.ci, 1)
 
     te.wait_ge(sem.cz, 1)
+    te.wait_ge(sem.cp, 2)
     for i in range(NB):
         te.matmul(ST[i][:, 0:2 * QP], T.zer[:], T.zer[:, 0:2 * QP], True, False)
     te.wait_ge(sem.ql, 16)
@@ -124,35 +128,34 @@ def _root(g, core, T, topo, others):
 
     ve.wait_ge(sem.sso, 1)
     ve.tensor_reduce(T.mg[0:QP, 0:1], S[0][0:QP, 0:KP], X, mx).then_inc(sem.smo, 1)
-    for s in range(NR - 1):
+    for s in range(NR - 2):
         ve.wait_ge(sem["ss%d" % s], 1)
         ve.tensor_reduce(T.mg[0:QP, s + 1:s + 2], sb(s), X, mx).then_inc(sem["rm%d" % s], 1)
+    ve.wait_ge(sem.cp, 2)
     ve.wait_ge(sem.smo, 1)
-    for s in range(NR - 1):
+    for s in range(NR - 2):
         ve.wait_ge(sem["rm%d" % s], 1)
-    ve.tensor_reduce(T.negm[0:QP, 0:1], T.mg[0:QP, 0:NR], X, mx, negate=True).then_inc(sem.sn, 1)
-    ve.wait_ge(sem.sn, 1)
-    ve.wait_ge(sem.ci, 1)
-    ve.tensor_scalar(T.diag[0:QP, 0:QP], T.I[0:QP, 0:QP], T.negm[0:QP, 0:1], None, mult).then_inc(sem.sd, 1)
+    ve.wait_ge(sem["ss%d" % (NR - 2)], 1)
+    ve.tensor_tensor_scan(T.Cb[0:QP, :], S[LB][0:QP, 0:2 * KP], T.mg[0:QP, :], LOW, mx, mx).then_inc(sem.sd, 1)
 
     te.wait_ge(sem.sd, 1)
-    te.wait_ge(sem.c1, 1)
+    te.wait_ge(sem.ci, 1)
     for i in range(NB):
         for s in (i, i + NB):
-            te.matmul(st(s), T.ones[0:QP, 0:128], T.diag[0:QP, 0:QP], False, s >= NB).then_inc(sem["st%d" % i], 1)
+            te.matmul(st(s), T.Cb[0:QP, KP:2 * KP], T.NI[0:QP, :], False, s >= NB).then_inc(sem["st%d" % i], 1)
     for i in range(NB):
         se.wait_ge(sem["st%d" % i], 2)
         se.activation(T.PT[:, 2 * i * QP:(2 * i + 2) * QP], ST[i][:, 0:2 * QP], Exp).then_inc(sem["sp%d" % i], 1)
 
     order = [s for i in range(NB) for s in (i, i + NB)]
-    te.wait_ge(sem.c2, NR)
     for n, s in enumerate(order):
         if s < NB:
             te.wait_ge(sem["sp%d" % s], 1)
         if s == OWN:
             te.wait_ge(sem.vl, 16)
+            te.wait_ge(sem.c2, 1)
         else:
-            te.wait_ge(sem["va%d" % s], eng[s])
+            te.wait_ge(sem["va%d" % s], 2 * eng[s])
         te.matmul(Olo[0:QP, 0:FH + 1], pt(s), T.Vlo[:, s * VS:s * VS + FH + 1], n == 0, n == NR - 1).then_inc(sem.slo, 1)
     for n, s in enumerate(order):
         if s == OWN:
@@ -166,10 +169,13 @@ def _root(g, core, T, topo, others):
     ve.wait_ge(sem.sr, 1)
     ve.tensor_scalar(T.yb[0:QP, 0:FH], Olo[0:QP, 0:FH], T.rl[0:QP, 0:1], None, mult).then_inc(sem.syb, 1)
     ve.wait_ge(sem.shi, NR)
-    ve.tensor_scalar(T.yb[0:QP, FH:F], Ohi[0:QP, 0:FH], T.rl[0:QP, 0:1], None, mult).then_inc(sem.syb, 1)
-    g.sync.wait_ge(sem.syb, 2)
-    g.sync.dma_start(T.y[:], T.yb[0:QP, :]).then_inc(sem.done, 16)
+    ve.tensor_scalar(T.yb[0:QP, FH:F], Ohi[0:QP, 0:FH], T.rl[0:QP, 0:1], None, mult).then_inc(sem.syh, 1)
+    se.wait_ge(sem.syb, 1)
+    se.dma_start(T.y[:, 0:FH], T.yb[0:QP, 0:FH]).then_inc(sem.done2, 16)
+    g.sync.wait_ge(sem.syh, 1)
+    g.sync.dma_start(T.y[:, FH:F], T.yb[0:QP, FH:F]).then_inc(sem.done, 16)
     g.sync.wait_ge(sem.done, 16)
+    se.wait_ge(sem.done2, 16)
 
 
 def rank_program(g, core, T, topo):

from concourse.mybir import AluOpType, AxisListType, ActivationFunctionType

KP, QP, F = 128, 64, 128
NR = 8
FH = F // 2
OWN = NR - 1
NB = 4
LOW = -1e29
OB = 8
VS = FH + OB

SCRATCH = {
    "kd": ("dram", [128, KP], "bfloat16"),
    "vs": ("sbuf", [128, F], "bfloat16"),
    "on": ("sbuf", [128, OB], "bfloat16"),
    "qs": ("sbuf", [128, QP], "bfloat16"),
    "K": ("sbuf", [128, NR * KP], "bfloat16"),
    "Vlo": ("sbuf", [128, NR * VS], "bfloat16"),
    "Vhi": ("sbuf", [128, NR * FH], "bfloat16"),
    "PT": ("sbuf", [128, NR * QP], "bfloat16"),
    "zer": ("sbuf", [128, 128], "bfloat16"),
    "ones": ("sbuf", [128, QP], "bfloat16"),
    "nones": ("sbuf", [128, QP], "bfloat16"),
    "NI": ("sbuf", [128, QP], "bfloat16"),
    "mg": ("sbuf", [128, 2 * KP], "float32"),
    "Cb": ("sbuf", [128, 2 * KP], "bfloat16"),
    "rl": ("sbuf", [128, 1], "float32"),
    "yb": ("sbuf", [128, F], "bfloat16"),
    "S0": ("psum", [128, 512], "float32"),
    "S1": ("psum", [128, 512], "float32"),
    "S2": ("psum", [128, 512], "float32"),
    "S3": ("psum", [128, 512], "float32"),
    "ST0": ("psum", [128, 512], "float32"),
    "ST1": ("psum", [128, 512], "float32"),
    "ST2": ("psum", [128, 512], "float32"),
    "ST3": ("psum", [128, 512], "float32"),
}
SEMAPHORES = (["ql", "kl", "vl", "vl2", "sent", "cz", "c1", "c2", "ci", "cn", "cp", "sso", "smo", "sd", "slo", "shi", "sr",
               "syb", "syh", "done", "done2"]
              + ["ka%d" % i for i in range(NR - 1)] + ["ss%d" % i for i in range(NR - 1)] + ["rm%d" % i for i in range(NR - 2)]
              + ["va%d" % i for i in range(NR - 1)] + ["vb%d" % i for i in range(NR - 1)]
              + ["st%d" % i for i in range(NB)] + ["sp%d" % i for i in range(NB)])


def _count(mask):
    return bin(mask).count("1")


def _sender(g, core, slot, T, topo, rc):
    sem = T.sem
    mask = topo.mask(core, rc)
    rid, pid = topo.addr(rc, core)
    g.sync.dma_start(T.kd[:], T.k[:]).then_inc(sem.kl, 16)
    g.sync.dma_start(T.vs[:], T.v[:]).then_inc(sem.vl, 16)
    g.vector.memset(T.on[:], 1.0).then_inc(sem.c2, 1)
    g.wait_ge(sem.c2, 1)
    g.remote_dma(out_ap=T.Vlo[:, slot * VS + FH:(slot + 1) * VS], in_ap=T.on[:], remote_sem=sem["va%d" % slot],
                 local_sem=sem.sent, pid=pid, routing_id=rid, dma_engine_mask=mask)
    g.wait_ge(sem.kl, 16)
    g.remote_dma(out_ap=T.K[:, slot * KP:(slot + 1) * KP], in_ap=T.kd[:], remote_sem=sem["ka%d" % slot],
                 local_sem=sem.sent, pid=pid, routing_id=rid, dma_engine_mask=mask)
    g.wait_ge(sem.vl, 16)
    g.remote_dma(out_ap=T.Vlo[:, slot * VS:slot * VS + FH], in_ap=T.vs[:, 0:FH], remote_sem=sem["va%d" % slot],
                 local_sem=sem.sent, pid=pid, routing_id=rid, dma_engine_mask=mask)
    g.remote_dma(out_ap=T.Vhi[:, slot * FH:(slot + 1) * FH], in_ap=T.vs[:, FH:F], remote_sem=sem["vb%d" % slot],
                 local_sem=sem.sent, pid=pid, routing_id=rid, dma_engine_mask=mask)
    g.wait_ge(sem.sent, 4 * _count(mask))


def _root(g, core, T, topo, others):
    sem = T.sem
    te, ve, se = g.tensor, g.vector, g.scalar
    Exp = ActivationFunctionType.Exp
    X, mx, mult = AxisListType.X, AluOpType.max, AluOpType.mult
    eng = [_count(topo.mask(T.cores[j], core)) for j in others]
    S = [T["S%d" % i] for i in range(NB)]
    ST = [T["ST%d" % i] for i in range(NB)]
    Olo, Ohi = S[1], S[2]
    LB = (NR - 1) % NB

    def sb(s):
        return S[(s + 1) % NB][0:QP, 0:KP]

    def st(s):
        c = (s // NB) * QP
        return ST[s % NB][:, c:c + QP]

    def pt(s):
        c = (2 * (s % NB) + s // NB) * QP
        return T.PT[:, c:c + QP]

    def ks(s):
        return T.K[:, s * KP:(s + 1) * KP]

    g.sync.dma_start(T.qs[:], T.q[:]).then_inc(sem.ql, 16)
    se.dma_start(ks(OWN), T.k[:]).then_inc(sem.kl, 16)
    g.sync.dma_start(T.Vlo[:, OWN * VS:OWN * VS + FH], T.v[:, 0:FH]).then_inc(sem.vl, 16)
    se.dma_start(T.Vhi[:, OWN * FH:(OWN + 1) * FH], T.v[:, FH:F]).then_inc(sem.vl2, 16)

    ve.memset(T.zer[:], 0.0).then_inc(sem.cz, 1)
    ve.memset(T.mg[0:QP, NR - 1:2 * KP], LOW).then_inc(sem.cp, 1)
    ve.memset(S[LB][0:QP, KP:2 * KP], LOW).then_inc(sem.cp, 1)
    ve.memset(T.Vlo[:, OWN * VS + FH:(OWN + 1) * VS], 1.0).then_inc(sem.c2, 1)
    se.wait_ge(sem.cz, 1)
    se.activation(T.ones[0:QP, :], T.zer[0:QP, 0:QP], Exp).then_inc(sem.c1, 1)
    ve.wait_ge(sem.c1, 1)
    ve.tensor_scalar(T.nones[0:QP, :], T.ones[0:QP, :], -1.0, None, mult).then_inc(sem.cn, 1)
    g.wait_ge(sem.cn, 1)
    g.affine_select(T.NI[0:QP, :], T.nones[0:QP, :], [[-1, QP]], AluOpType.is_equal, 0.0, 0, 1).then_inc(sem.ci, 1)

    te.wait_ge(sem.cz, 1)
    te.wait_ge(sem.cp, 2)
    for i in range(NB):
        te.matmul(ST[i][:, 0:2 * QP], T.zer[:], T.zer[:, 0:2 * QP], True, False)
    te.wait_ge(sem.ql, 16)
    te.wait_ge(sem.kl, 16)
    te.matmul(S[0][0:QP, 0:KP], T.qs[:], ks(OWN), True, True).then_inc(sem.sso, 1)
    te.matmul(st(OWN), ks(OWN), T.qs[:], False, False)
    for s in range(NR - 1):
        te.wait_ge(sem["ka%d" % s], eng[s])
        if s == NB - 1:
            te.wait_ge(sem.smo, 1)
        elif s >= NB:
            te.wait_ge(sem["rm%d" % (s - NB)], 1)
        te.matmul(sb(s), T.qs[:], ks(s), True, True).then_inc(sem["ss%d" % s], 1)
    for s in range(NR - 1):
        te.matmul(st(s), ks(s), T.qs[:], False, False)

    ve.wait_ge(sem.sso, 1)
    ve.tensor_reduce(T.mg[0:QP, 0:1], S[0][0:QP, 0:KP], X, mx).then_inc(sem.smo, 1)
    for s in range(NR - 2):
        ve.wait_ge(sem["ss%d" % s], 1)
        ve.tensor_reduce(T.mg[0:QP, s + 1:s + 2], sb(s), X, mx).then_inc(sem["rm%d" % s], 1)
    ve.wait_ge(sem.cp, 2)
    ve.wait_ge(sem.smo, 1)
    for s in range(NR - 2):
        ve.wait_ge(sem["rm%d" % s], 1)
    ve.wait_ge(sem["ss%d" % (NR - 2)], 1)
    ve.tensor_tensor_scan(T.Cb[0:QP, :], S[LB][0:QP, 0:2 * KP], T.mg[0:QP, :], LOW, mx, mx).then_inc(sem.sd, 1)

    te.wait_ge(sem.sd, 1)
    te.wait_ge(sem.ci, 1)
    for i in range(NB):
        for s in (i, i + NB):
            te.matmul(st(s), T.Cb[0:QP, KP:2 * KP], T.NI[0:QP, :], False, s >= NB).then_inc(sem["st%d" % i], 1)
    for i in range(NB):
        se.wait_ge(sem["st%d" % i], 2)
        se.activation(T.PT[:, 2 * i * QP:(2 * i + 2) * QP], ST[i][:, 0:2 * QP], Exp).then_inc(sem["sp%d" % i], 1)

    order = [s for i in range(NB) for s in (i, i + NB)]
    for n, s in enumerate(order):
        if s < NB:
            te.wait_ge(sem["sp%d" % s], 1)
        if s == OWN:
            te.wait_ge(sem.vl, 16)
            te.wait_ge(sem.c2, 1)
        else:
            te.wait_ge(sem["va%d" % s], 2 * eng[s])
        te.matmul(Olo[0:QP, 0:FH + 1], pt(s), T.Vlo[:, s * VS:s * VS + FH + 1], n == 0, n == NR - 1).then_inc(sem.slo, 1)
    for n, s in enumerate(order):
        if s == OWN:
            te.wait_ge(sem.vl2, 16)
        else:
            te.wait_ge(sem["vb%d" % s], eng[s])
        te.matmul(Ohi[0:QP, 0:FH], pt(s), T.Vhi[:, s * FH:(s + 1) * FH], n == 0, n == NR - 1).then_inc(sem.shi, 1)

    ve.wait_ge(sem.slo, NR)
    ve.reciprocal(T.rl[0:QP, 0:1], Olo[0:QP, FH:FH + 1]).then_inc(sem.sr, 1)
    ve.wait_ge(sem.sr, 1)
    ve.tensor_scalar(T.yb[0:QP, 0:FH], Olo[0:QP, 0:FH], T.rl[0:QP, 0:1], None, mult).then_inc(sem.syb, 1)
    ve.wait_ge(sem.shi, NR)
    ve.tensor_scalar(T.yb[0:QP, FH:F], Ohi[0:QP, 0:FH], T.rl[0:QP, 0:1], None, mult).then_inc(sem.syh, 1)
    se.wait_ge(sem.syb, 1)
    se.dma_start(T.y[:, 0:FH], T.yb[0:QP, 0:FH]).then_inc(sem.done2, 16)
    g.sync.wait_ge(sem.syh, 1)
    g.sync.dma_start(T.y[:, FH:F], T.yb[0:QP, FH:F]).then_inc(sem.done, 16)
    g.sync.wait_ge(sem.done, 16)
    se.wait_ge(sem.done2, 16)


def rank_program(g, core, T, topo):
    rank = T.rank_of(core)
    if rank is None:
        return
    others = [j for j in range(NR) if j != T.root]
    if rank == T.root:
        _root(g, core, T, topo, others)
    else:
        _sender(g, core, others.index(rank), T, topo, T.cores[T.root])
